import numpy as np
import ml_dtypes

BF16 = ml_dtypes.bfloat16


def bf(x):
    return np.asarray(x, np.float32).astype(BF16)


def f32(x):
    return np.asarray(x, np.float32)


def f64(x):
    return np.asarray(x).astype(np.float64)


def striped(idx):
    return np.concatenate([l.reshape(-1, 16).T for l in idx])


def rows(idx, k):
    return np.tile(np.repeat(idx, 16, axis=0), (k // (16 * 8), 1))


def look(tab, idx):
    return np.take_along_axis(f64(tab), rows(idx, len(tab)), axis=1)


K, S, V, N, M = 128, 2048, 1024, 1024, 256


def setup_inputs():
    return {"tab": bf(np.random.standard_normal((K, S))), "w": bf(np.random.standard_normal((K, M)) / np.sqrt(K)), "b": f32(0.5 * np.random.standard_normal((M, 1))), "offs": striped(np.random.randint(0, S, (8, N)))}


def reference(tab, w, b, offs):
    idx = np.stack([g.T.reshape(-1) for g in np.split(offs, 8)])
    t = look(tab, idx)
    x = t
    y = f64(w).T @ x
    return np.maximum(y + f64(b), 0.0)

@@ -1,0 +1,43 @@
+import concourse.mybir as mybir
+
+BF16, F32, U16 = mybir.dt.bfloat16, mybir.dt.float32, mybir.dt.uint16
+RELU = mybir.ActivationFunctionType.Relu
+
+P = 128
+GROUP = 16
+PIECE = 512
+
+FLOPS = 2 * 128 * 256 * 1024
+
+
+def tile_lookup_dec_copy_relu_kernel(tc, tab, w, b, offs, out):
+    nc = tc.nc
+    codewords = tab.shape[1]
+    features, vectors = out.shape
+    blocks = features // P
+
+    out_rows = out.rearrange("(p i) n -> p i n", i=blocks)
+
+    with (
+        tc.tile_pool(name="held", bufs=1) as held,
+        tc.psum_pool(name="psum", bufs=1) as psum,
+    ):
+        offsets = held.tile([P, vectors // GROUP], U16, name="offsets")
+        table = held.tile([P, codewords], BF16, name="table")
+        weights = held.tile([P, P, blocks], BF16, name="weights")
+        bias = held.tile([P, blocks], F32, name="bias")
+        nc.sync.dma_start(offsets[:], offs)
+        nc.sync.dma_start(table[:], tab)
+        nc.sync.dma_start(weights[:], w.rearrange("r (p i) -> r p i", i=blocks))
+        nc.sync.dma_start(bias[:], b.rearrange("(p i) o -> p (i o)", i=blocks))
+
+        for c in range(vectors // PIECE):
+            picked = held.tile([P, PIECE], BF16, name=f"picked{c}")
+            piece_offsets = offsets[:, c * PIECE // GROUP : (c + 1) * PIECE // GROUP]
+            nc.vector.tensor_copy(picked[:], table[:].indirect(piece_offsets))
+            for i in range(blocks):
+                product = psum.tile([P, PIECE], F32, name=f"product{c}_{i}")
+                result = held.tile([P, PIECE], F32, name=f"result{c}_{i}")
+                nc.tensor.matmul(product[:], weights[:, :, i], picked[:])
+                nc.scalar.activation(result[:], product[:], RELU, bias=bias[:, i : i + 1])
+                nc.sync.dma_start(out_rows[:, i, c * PIECE : (c + 1) * PIECE], result[:])

@@ -2,10 +2,12 @@ import concourse.mybir as mybir
 
 BF16, F32, U16 = mybir.dt.bfloat16, mybir.dt.float32, mybir.dt.uint16
 RELU = mybir.ActivationFunctionType.Relu
+ADD, MAX = mybir.AluOpType.add, mybir.AluOpType.max
 
 P = 128
 GROUP = 16
 PIECE = 512
+CHUNK = 256
 
 FLOPS = 2 * 128 * 256 * 1024
 
@@ -15,6 +17,7 @@ def tile_lookup_dec_copy_relu_kernel(tc, tab, w, b, offs, out):
     codewords = tab.shape[1]
     features, vectors = out.shape
     blocks = features // P
+    pieces = vectors // PIECE
 
     out_rows = out.rearrange("(p i) n -> p i n", i=blocks)
 
@@ -26,18 +29,25 @@ def tile_lookup_dec_copy_relu_kernel(tc, tab, w, b, offs, out):
         table = held.tile([P, codewords], BF16, name="table")
         weights = held.tile([P, P, blocks], BF16, name="weights")
         bias = held.tile([P, blocks], F32, name="bias")
-        nc.sync.dma_start(offsets[:], offs)
         nc.sync.dma_start(table[:], tab)
+        nc.sync.dma_start(offsets[:], offs)
         nc.sync.dma_start(weights[:], w.rearrange("r (p i) -> r p i", i=blocks))
-        nc.sync.dma_start(bias[:], b.rearrange("(p i) o -> p (i o)", i=blocks))
+        nc.scalar.dma_start(bias[:], b.rearrange("(p i) o -> p (i o)", i=blocks))
 
-        for c in range(vectors // PIECE):
-            picked = held.tile([P, PIECE], BF16, name=f"picked{c}")
+        picked = [held.tile([P, PIECE], BF16, name=f"picked{c}") for c in range(pieces)]
+        for c in range(pieces):
             piece_offsets = offsets[:, c * PIECE // GROUP : (c + 1) * PIECE // GROUP]
-            nc.vector.tensor_copy(picked[:], table[:].indirect(piece_offsets))
+            nc.vector.tensor_copy(picked[c][:], table[:].indirect(piece_offsets))
+
+        for c in range(pieces):
             for i in range(blocks):
-                product = psum.tile([P, PIECE], F32, name=f"product{c}_{i}")
-                result = held.tile([P, PIECE], F32, name=f"result{c}_{i}")
-                nc.tensor.matmul(product[:], weights[:, :, i], picked[:])
-                nc.scalar.activation(result[:], product[:], RELU, bias=bias[:, i : i + 1])
-                nc.sync.dma_start(out_rows[:, i, c * PIECE : (c + 1) * PIECE], result[:])
+                for h in range(PIECE // CHUNK):
+                    product = psum.tile([P, CHUNK], F32, name=f"product{c}_{i}_{h}")
+                    result = held.tile([P, CHUNK], F32, name=f"result{c}_{i}_{h}")
+                    nc.tensor.matmul(product[:], weights[:, :, i], picked[c][:, h * CHUNK : (h + 1) * CHUNK])
+                    if c == pieces - 1 and h % 2 == 0:
+                        nc.vector.tensor_scalar(result[:], product[:], bias[:, i : i + 1], 0.0, ADD, MAX)
+                    else:
+                        nc.scalar.activation(result[:], product[:], RELU, bias=bias[:, i : i + 1])
+                    first = c * PIECE + h * CHUNK
+                    nc.sync.dma_start(out_rows[:, i, first : first + CHUNK], result[:])

@@ -8,6 +8,8 @@ P = 128
 GROUP = 16
 PIECE = 512
 CHUNK = 256
+WARM_DURING_LOADS = 8
+WARM_DURING_GATHER = 4
 
 FLOPS = 2 * 128 * 256 * 1024
 
@@ -32,7 +34,24 @@ def tile_lookup_dec_copy_relu_kernel(tc, tab, w, b, offs, out):
         nc.sync.dma_start(table[:], tab)
         nc.sync.dma_start(offsets[:], offs)
         nc.sync.dma_start(weights[:], w.rearrange("r (p i) -> r p i", i=blocks))
-        nc.scalar.dma_start(bias[:], b.rearrange("(p i) o -> p (i o)", i=blocks))
+        nc.sync.dma_start(bias[:], b.rearrange("(p i) o -> p (i o)", i=blocks))
+
+        products = {
+            (c, h, i): psum.tile([P, CHUNK], F32, name=f"product{c}_{h}_{i}")
+            for c in range(pieces)
+            for h in range(PIECE // CHUNK)
+            for i in range(blocks)
+        }
+
+        zeros = held.tile([P, CHUNK], BF16, name="zeros")
+        warmed = held.tile([P, 1], F32, name="warmed")
+        nc.vector.memset(zeros[:], 0.0)
+        nc.scalar.activation(warmed[:], zeros[:, 0:1], RELU)
+        warm_bank = products[pieces - 1, PIECE // CHUNK - 1, blocks - 1]
+        for k in range(WARM_DURING_LOADS):
+            nc.tensor.matmul(warm_bank[:], zeros[:, 0:P], zeros[:])
+        for k in range(WARM_DURING_GATHER):
+            nc.tensor.matmul(warm_bank[:], zeros[:, 0:P], weights[:].rearrange("r p i -> r (p i)"))
 
         picked = [held.tile([P, PIECE], BF16, name=f"picked{c}") for c in range(pieces)]
         for c in range(pieces):
@@ -40,14 +59,18 @@ def tile_lookup_dec_copy_relu_kernel(tc, tab, w, b, offs, out):
             nc.vector.tensor_copy(picked[c][:], table[:].indirect(piece_offsets))
 
         for c in range(pieces):
-            for i in range(blocks):
-                for h in range(PIECE // CHUNK):
-                    product = psum.tile([P, CHUNK], F32, name=f"product{c}_{i}_{h}")
-                    result = held.tile([P, CHUNK], F32, name=f"result{c}_{i}_{h}")
+            last_piece = c == pieces - 1
+            for h in range(PIECE // CHUNK):
+                columns = slice(c * PIECE + h * CHUNK, c * PIECE + (h + 1) * CHUNK)
+                result = held.tile([P, blocks, CHUNK], F32, name=f"result{c}_{h}")
+                for i in range(blocks):
+                    product = products[c, h, i]
                     nc.tensor.matmul(product[:], weights[:, :, i], picked[c][:, h * CHUNK : (h + 1) * CHUNK])
-                    if c == pieces - 1 and h % 2 == 0:
-                        nc.vector.tensor_scalar(result[:], product[:], bias[:, i : i + 1], 0.0, ADD, MAX)
+                    if last_piece and i % 2 == 0:
+                        nc.vector.tensor_scalar(result[:, i, :], product[:], bias[:, i : i + 1], 0.0, ADD, MAX)
                     else:
-                        nc.scalar.activation(result[:], product[:], RELU, bias=bias[:, i : i + 1])
-                    first = c * PIECE + h * CHUNK
-                    nc.sync.dma_start(out_rows[:, i, first : first + CHUNK], result[:])
+                        nc.scalar.activation(result[:, i, :], product[:], RELU, bias=bias[:, i : i + 1])
+                    if not last_piece:
+                        nc.sync.dma_start(out_rows[:, i, columns], result[:, i, :])
+                if last_piece:
+                    nc.sync.dma_start(out_rows[:, :, columns], result[:])

@@ -60,17 +60,18 @@ def tile_lookup_dec_copy_relu_kernel(tc, tab, w, b, offs, out):
 
         for c in range(pieces):
             last_piece = c == pieces - 1
-            for h in range(PIECE // CHUNK):
-                columns = slice(c * PIECE + h * CHUNK, c * PIECE + (h + 1) * CHUNK)
-                result = held.tile([P, blocks, CHUNK], F32, name=f"result{c}_{h}")
-                for i in range(blocks):
+            for i in range(blocks):
+                result = held.tile([P, PIECE], F32, name=f"result{c}_{i}")
+                out_piece = out_rows[:, i, c * PIECE : (c + 1) * PIECE]
+                for h in range(PIECE // CHUNK):
+                    columns = slice(h * CHUNK, (h + 1) * CHUNK)
                     product = products[c, h, i]
-                    nc.tensor.matmul(product[:], weights[:, :, i], picked[c][:, h * CHUNK : (h + 1) * CHUNK])
-                    if last_piece and i % 2 == 0:
-                        nc.vector.tensor_scalar(result[:, i, :], product[:], bias[:, i : i + 1], 0.0, ADD, MAX)
+                    nc.tensor.matmul(product[:], weights[:, :, i], picked[c][:, columns])
+                    if last_piece and h % 2 == 0:
+                        nc.vector.tensor_scalar(result[:, columns], product[:], bias[:, i : i + 1], 0.0, ADD, MAX)
                     else:
-                        nc.scalar.activation(result[:, i, :], product[:], RELU, bias=bias[:, i : i + 1])
+                        nc.scalar.activation(result[:, columns], product[:], RELU, bias=bias[:, i : i + 1])
                     if not last_piece:
-                        nc.sync.dma_start(out_rows[:, i, columns], result[:, i, :])
+                        nc.sync.dma_start(out_piece[:, columns], result[:, columns])
                 if last_piece:
-                    nc.sync.dma_start(out_rows[:, :, columns], result[:])
+                    nc.sync.dma_start(out_piece, result[:])

import concourse.mybir as mybir

BF16, F32, U16 = mybir.dt.bfloat16, mybir.dt.float32, mybir.dt.uint16
RELU = mybir.ActivationFunctionType.Relu
ADD, MAX = mybir.AluOpType.add, mybir.AluOpType.max

P = 128
GROUP = 16
PIECE = 512
CHUNK = 256
WARM_DURING_LOADS = 8
WARM_DURING_GATHER = 4

FLOPS = 2 * 128 * 256 * 1024


def tile_lookup_dec_copy_relu_kernel(tc, tab, w, b, offs, out):
    nc = tc.nc
    codewords = tab.shape[1]
    features, vectors = out.shape
    blocks = features // P
    pieces = vectors // PIECE

    out_rows = out.rearrange("(p i) n -> p i n", i=blocks)

    with (
        tc.tile_pool(name="held", bufs=1) as held,
        tc.psum_pool(name="psum", bufs=1) as psum,
    ):
        offsets = held.tile([P, vectors // GROUP], U16, name="offsets")
        table = held.tile([P, codewords], BF16, name="table")
        weights = held.tile([P, P, blocks], BF16, name="weights")
        bias = held.tile([P, blocks], F32, name="bias")
        nc.sync.dma_start(table[:], tab)
        nc.sync.dma_start(offsets[:], offs)
        nc.sync.dma_start(weights[:], w.rearrange("r (p i) -> r p i", i=blocks))
        nc.sync.dma_start(bias[:], b.rearrange("(p i) o -> p (i o)", i=blocks))

        products = {
            (c, h, i): psum.tile([P, CHUNK], F32, name=f"product{c}_{h}_{i}")
            for c in range(pieces)
            for h in range(PIECE // CHUNK)
            for i in range(blocks)
        }

        zeros = held.tile([P, CHUNK], BF16, name="zeros")
        warmed = held.tile([P, 1], F32, name="warmed")
        nc.vector.memset(zeros[:], 0.0)
        nc.scalar.activation(warmed[:], zeros[:, 0:1], RELU)
        warm_bank = products[pieces - 1, PIECE // CHUNK - 1, blocks - 1]
        for k in range(WARM_DURING_LOADS):
            nc.tensor.matmul(warm_bank[:], zeros[:, 0:P], zeros[:])
        for k in range(WARM_DURING_GATHER):
            nc.tensor.matmul(warm_bank[:], zeros[:, 0:P], weights[:].rearrange("r p i -> r (p i)"))

        picked = [held.tile([P, PIECE], BF16, name=f"picked{c}") for c in range(pieces)]
        for c in range(pieces):
            piece_offsets = offsets[:, c * PIECE // GROUP : (c + 1) * PIECE // GROUP]
            nc.vector.tensor_copy(picked[c][:], table[:].indirect(piece_offsets))

        for c in range(pieces):
            last_piece = c == pieces - 1
            for i in range(blocks):
                result = held.tile([P, PIECE], F32, name=f"result{c}_{i}")
                out_piece = out_rows[:, i, c * PIECE : (c + 1) * PIECE]
                for h in range(PIECE // CHUNK):
                    columns = slice(h * CHUNK, (h + 1) * CHUNK)
                    product = products[c, h, i]
                    nc.tensor.matmul(product[:], weights[:, :, i], picked[c][:, columns])
                    if last_piece and h % 2 == 0:
                        nc.vector.tensor_scalar(result[:, columns], product[:], bias[:, i : i + 1], 0.0, ADD, MAX)
                    else:
                        nc.scalar.activation(result[:, columns], product[:], RELU, bias=bias[:, i : i + 1])
                    if not last_piece:
                        nc.sync.dma_start(out_piece[:, columns], result[:, columns])
                if last_piece:
                    nc.sync.dma_start(out_piece, result[:])
